import numpy as np
import ml_dtypes


def mxq(x, axis, fmt="e4m3"):
    dtype, down = {"e4m3": (ml_dtypes.float8_e4m3fn, 7), "e5m2": (ml_dtypes.float8_e5m2, 14)}[fmt]
    v = np.moveaxis(np.asarray(x, np.float32).astype(ml_dtypes.bfloat16).astype(np.float64), axis, -1)
    blocks = v.reshape(v.shape[:-1] + (-1, 32))
    amax = np.abs(blocks).max(-1, keepdims=True)
    byte = np.maximum(np.where(amax > 0, np.frexp(amax)[1] - 1 + 127, 0) - down, 1)
    scale = np.exp2(byte - 127.0)
    codes = (blocks / scale).astype(np.float32).astype(dtype).astype(np.float64)
    return np.moveaxis((codes * scale).reshape(v.shape), -1, axis)


WIDE = False


def mx_kscale(k):
    if not WIDE:
        return np.ones(k)
    levels = np.array([10, -10, 5, -5, 0])
    if k % 512:
        return np.exp2(np.random.permutation(np.resize(levels, k // 32))).repeat(32)
    a = np.empty((k // 512, 16))
    for p in range(k // 512):
        a[p, :8] = np.random.permutation(np.resize(levels, 8))
        for g in range(8):
            far = levels[np.abs(levels - a[p, g]) >= 10]
            a[p, g + 8] = far[np.random.randint(len(far))]
    return np.exp2(a.ravel()).repeat(32)


BF16 = ml_dtypes.bfloat16


def bf(x):
    return np.asarray(x, np.float32).astype(BF16)


def f64(x):
    return np.asarray(x).astype(np.float64)

def planes(Y):
    n, m = Y.shape
    b = f64(bf(Y)).reshape(n // 32, 32, m)
    amax = np.abs(b).max(1)
    byte = np.clip(np.where(amax > 0, np.frexp(amax)[1] - 1 + 127 - 7, 1), 1, 254)
    codes = (b * np.exp2(127.0 - byte)[:, None, :]).reshape(n, m).astype(np.float32).astype(ml_dtypes.float8_e4m3fn).view(np.uint8)
    words = codes.reshape(n // 512, 128, 4, m).transpose(0, 1, 3, 2)
    return np.ascontiguousarray(words), np.ascontiguousarray(byte.astype(np.uint8).reshape(n // 512, 16, m))


B, D, K = 1024, 1024, 1024


def setup_inputs():
    s, t = mx_kscale(D), mx_kscale(B)
    return {
        "x": bf(np.random.standard_normal((B, D)) * s),
        "xn": bf(np.random.standard_normal((B, D)) * s),
        "w": bf(np.random.standard_normal((D, K)) / np.sqrt(D) / s[:, None]),
        "emph": bf(np.random.uniform(0.5, 1.5, B) * t),
        "rho": bf(np.random.uniform(0.5, 1.5, B) / t),
        "gamma": bf(np.random.uniform(0.7, 1.0, B)),
    }


def core(x, xn, w, emph, rho, gamma):
    batch = x.shape[0]
    wq = mxq(f64(w), 0, "e4m3")
    phi = np.tanh(mxq(f64(x), 1, "e4m3") @ wq)
    phin = np.tanh(mxq(f64(xn), 1, "e4m3") @ wq)
    left = f64(emph)[:, None] * phi
    right = f64(rho)[:, None] * (phi - f64(gamma)[:, None] * phin)
    return (mxq(left, 0, "e4m3").T @ mxq(right, 0, "e4m3")) / np.sqrt(batch)


def reference(x, xn, w, emph, rho, gamma):
    R_out = core(x, xn, w, emph, rho, gamma)
    words, scales = planes(R_out.T)
    return R_out, words, scales

from contextlib import ExitStack

import concourse.mybir as mybir
from concourse.masks import make_identity

F32 = mybir.dt.float32
BF16 = mybir.dt.bfloat16
U32 = mybir.dt.uint32
I32 = mybir.dt.int32
U8 = mybir.dt.uint8
E4M3 = mybir.dt.float8_e4m3fn_x4
MULT = mybir.AluOpType.mult
ADD = mybir.AluOpType.add
COPY = mybir.ActivationFunctionType.Copy
TANH = mybir.ActivationFunctionType.Tanh

N = 1024
P = 128
T = 4
GROUP = P * T
GROUPS = N // GROUP
PART = 256
FLOPS = 3 * 2 * N * N * N

LOADS = [
    ("x", 0, 2), ("x", 0, 3), ("w", 0, 0), ("w", 0, 1), ("x", 0, 0), ("x", 0, 1), ("n", 0, 2), ("n", 0, 3),
    ("w", 1, 0), ("w", 1, 1), ("n", 0, 0), ("n", 0, 1), ("x", 1, 2), ("emph",), ("x", 1, 1), ("x", 1, 3),
    ("x", 1, 0), ("gamma",), ("rho",), ("n", 1, 1), ("n", 1, 0), ("n", 1, 2), ("n", 1, 3),
]

STEPS = [
    ("turn", "x", 0, 1, "sv"), ("lay_w", 0, 0, "vs"), ("lay_w", 0, 1, "vs"), ("quant_x", "x", 0, 1),
    ("turn", "x", 0, 0, "vs"), ("turn", "n", 0, 1, "ss"), ("quant_w", 0, 0), ("quant_w", 0, 1),
    ("quant_x", "x", 0, 0), ("lay_w", 1, 0, "vs"), ("phi", "x", 0, 0, 1), ("quant_x", "n", 0, 1),
    ("lay_w", 1, 1, "vv"), ("phi", "x", 0, 0, 0), ("quant_w", 1, 0), ("turn", "n", 0, 0, "ss"), ("quant_w", 1, 1),
    ("phi", "n", 0, 0, 1), ("left", 0, 0, 1), ("quant_x", "n", 0, 0), ("turn", "x", 1, 1, "ss"),
    ("phi", "n", 0, 0, 0), ("turn", "x", 1, 0, "ss"), ("left", 0, 0, 0), ("quant_left", 0, 0, 1),
    ("prepare_factors",), ("turn", "n", 1, 0, "ss"), ("quant_left", 0, 0, 0), ("quant_x", "x", 1, 1),
    ("diff", 0, 0, 0), ("diff", 0, 0, 1), ("turn", "n", 1, 1, "ss"), ("quant_x", "x", 1, 0), ("phi", "x", 0, 1, 1),
    ("phi", "x", 0, 1, 0), ("right", 0, 0), ("phi", "x", 1, 1, 1), ("phi", "x", 1, 1, 0), ("quant_x", "n", 1, 1),
    ("quant_x", "n", 1, 0), ("phi", "n", 0, 1, 1), ("phi", "n", 0, 1, 0), ("left", 0, 1, 0), ("quant_right", 0, 0),
    ("left", 0, 1, 1), ("phi", "x", 1, 0, 1), ("quant_left", 0, 1, 0), ("phi", "x", 1, 0, 0), ("diff", 0, 1, 1),
    ("left", 1, 1, 0), ("diff", 0, 1, 0), ("weigh_right", 0, 1), ("quant_left", 0, 1, 1), ("left", 1, 1, 1),
    ("left", 1, 0, 0), ("right", 0, 1), ("quant_left", 1, 1, 0), ("phi", "n", 1, 0, 0), ("phi", "n", 1, 0, 1),
    ("phi", "n", 1, 1, 1), ("quant_left", 1, 0, 0), ("quant_right", 0, 1), ("diff", 1, 0, 0), ("left", 1, 0, 1),
    ("quant_left", 1, 1, 1), ("phi", "n", 1, 1, 0), ("flipped", 0, 5, "s"), ("diff", 1, 0, 1),
    ("flipped", 0, 1, "s"), ("flipped", 0, 0, "s"), ("flipped", 0, 4, "s"), ("flipped", 0, 3, "s"),
    ("main", 3, 0, "s"), ("main", 0, 0, "s"), ("quant_left", 1, 0, 1), ("diff", 1, 1, 0), ("diff", 1, 1, 1),
    ("weigh_right", 1, 1), ("flipped", 0, 7, "s"), ("right", 1, 0), ("main", 7, 0, "s"), ("main", 1, 0, "s"),
    ("right", 1, 1), ("quant_right", 1, 0), ("flipped", 0, 6, "s"), ("flipped", 0, 2, "s"), ("quant_right", 1, 1),
    ("quant_p", 0, 2), ("quant_p", 0, 1), ("main", 4, 0, "s"), ("quant_p", 0, 0), ("quant_p", 0, 3),
    ("main", 6, 0, "s"), ("main", 5, 0, "s"), ("main", 2, 0, "s"), ("store_p", 0, 0), ("main", 4, 1, "v"),
    ("flipped", 1, 0, "s"), ("flipped", 1, 3, "s"), ("flipped", 1, 2, "v"), ("flipped", 1, 1, "s"),
    ("main", 7, 1, "s"), ("main", 5, 1, "s"), ("flipped", 1, 7, "s"), ("flipped", 1, 6, "s"), ("store_p", 0, 1),
    ("quant_p", 1, 1), ("main", 1, 1, "s"), ("main", 0, 1, "s"), ("quant_p", 1, 0), ("main", 6, 1, "s"),
    ("store_p", 1, 0), ("quant_p", 1, 3), ("main", 2, 1, "s"), ("flipped", 1, 5, "s"), ("main", 3, 1, "s"),
    ("flipped", 1, 4, "s"), ("quant_p", 1, 2), ("store_p", 1, 1),
]


def tile_emphaticlstdkeymatrix_x1_kernel(tc, x, xn, w, emph, rho, gamma, out_0, out_1, out_2):
    nc = tc.nc
    with ExitStack() as ctx:
        keep = ctx.enter_context(tc.tile_pool(name="keep", bufs=1))
        two = ctx.enter_context(tc.tile_pool(name="two", bufs=2))
        four = ctx.enter_context(tc.tile_pool(name="four", bufs=4))
        five = ctx.enter_context(tc.tile_pool(name="five", bufs=5))
        banks = ctx.enter_context(tc.psum_pool(name="banks", bufs=8))

        ident = keep.tile([P, P], F32, name="ident", align_bytes=64)
        make_identity(nc, ident[:])

        factors = {}

        def load_factor(label):
            factors[label] = keep.tile([P, GROUPS, T], BF16, name=label + "_b")
            vector = {"emph": emph, "rho": rho, "gamma": gamma}[label]
            nc.sync.dma_start(out=factors[label][:], in_=vector.rearrange("(g m t) -> m g t", g=GROUPS, t=T))

        minus_gamma = keep.tile([P, GROUPS * T], F32, name="minus_gamma")
        rho_f = keep.tile([P, GROUPS * T], F32, name="rho_f")

        def prepare_factors():
            nc.vector.tensor_scalar_mul(minus_gamma[:], factors["gamma"][:].rearrange("m g t -> m (g t)"), -1.0)
            nc.vector.tensor_copy(out=rho_f[:], in_=factors["rho"][:].rearrange("m g t -> m (g t)"))

        raw, w_raw = {}, {}
        rows_of = {"x": x, "n": xn}

        def load_w(h, c):
            w_raw[h, c] = keep.tile([P, T, GROUP], BF16, name=f"w_raw_{h}{c}", align_bytes=64)
            block = w[GROUP * c : GROUP * c + GROUP, GROUP * h : GROUP * h + GROUP]
            nc.sync.dma_start(out=w_raw[h, c][:], in_=block.rearrange("(p j) f -> p j f", j=T))

        def load_rows(X, g, t):
            key = (X, g, t // 2)
            if key not in raw:
                raw[key] = keep.tile([P, 2, N], BF16, name=f"raw_{X}{g}{t // 2}", align_bytes=64)
            rows = rows_of[X].rearrange("(g m t) d -> g m t d", g=GROUPS, t=T)[g]
            nc.sync.dma_start(out=raw[key][:, t % 2, :], in_=rows[:, t, :])

        for what, *where in LOADS:
            if what == "w":
                load_w(*where)
            elif what in rows_of:
                load_rows(what, *where)
            else:
                load_factor(what)

        def codes_and_scales(words, label):
            codes = keep.tile([P, words], U32, name="codes_" + label, align_bytes=64)
            scales = keep.tile([P, words], U8, name="scales_" + label, align_bytes=64)
            return codes, scales

        def quantize(codes, scales, values):
            nc.vector.quantize_mx(out=codes.bitcast(E4M3), scales=scales, in_=values)

        def multiply(out, stationary, s_cols, moving, m_cols, first, last):
            nc.tensor.matmul_mx(
                out=out,
                lhsT=stationary[0][:, s_cols].bitcast(E4M3),
                lhsT_scale=stationary[1][:, s_cols],
                rhs=moving[0][:, m_cols].bitcast(E4M3),
                rhs_scale=moving[1][:, m_cols],
                start=first,
                stop=last,
            )


        x_values, x_q = {}, {}

        def turn(X, g, pair, engines):
            values = four.tile([P, 2, GROUPS, P, T], BF16, name="x_values", align_bytes=64)
            x_values[X, g, pair] = values
            words = raw[X, g, pair][:].rearrange("m t d -> m (t d)").bitcast(F32)
            for t in range(2):
                bank = banks.tile([P, GROUPS, 2, P], F32, name="bank")
                for c in range(GROUPS):
                    for u in range(2):
                        begin = N // 2 * t + GROUP // 2 * c + u
                        nc.tensor.transpose(bank[:, c, u, :], words[:, begin : begin + GROUP // 2 - 1 : 2], ident[:])
                target = values[:, t].rearrange("p c m e -> p (c m e)").bitcast(F32)
                target = target.rearrange("p (c m u) -> p c m u", c=GROUPS, u=2)
                source = bank[:].rearrange("p c u m -> p c m u")
                if engines[t] == "s":
                    nc.scalar.copy(out=target, in_=source)
                else:
                    nc.vector.tensor_copy(out=target, in_=source)

        def quant_x(X, g, pair):
            x_q[X, g, pair] = codes_and_scales(2 * GROUPS * P, f"x_{X}{g}{pair}")
            codes, scales = x_q[X, g, pair]
            quantize(codes[:], scales[:], x_values[X, g, pair][:].rearrange("p t c m e -> p (t c m e)"))


        w_values, w_q = {}, {}

        def lay_w(h, c, engines):
            values = two.tile([P, GROUP, T], BF16, name="w_values", align_bytes=64)
            w_values[h, c] = values
            for half in range(2):
                cols = slice(PART * half, PART * half + PART)
                target = values[:, cols, :].rearrange("p (f i) j -> p f j i", i=4)
                source = w_raw[h, c][:, :, cols].rearrange("p j (f i) -> p f j i", i=4)
                if engines[half] == "s":
                    nc.scalar.copy(out=target, in_=source)
                else:
                    nc.vector.tensor_copy(out=target, in_=source)

        def quant_w(h, c):
            w_q[h, c] = codes_and_scales(GROUP, f"w_{h}{c}")
            codes, scales = w_q[h, c]
            quantize(codes[:], scales[:], w_values[h, c][:].rearrange("p f j -> p (f j)"))


        act = {}

        def phi(X, h, g, pair):
            if (X, h, g) not in act:
                act[X, h, g] = keep.tile([P, T, GROUP], F32, name=f"act_{X}{h}{g}", align_bytes=64)
            for t in range(2):
                bank = banks.tile([P, GROUP], F32, name="bank")
                for c in range(GROUPS):
                    cols = slice(P * (GROUPS * t + c), P * (GROUPS * t + c) + P)
                    multiply(bank[:], x_q[X, g, pair], cols, w_q[h, c], slice(0, GROUP), c == 0, c == GROUPS - 1)
                nc.scalar.activation(out=act[X, h, g][:, 2 * pair + t, :], in_=bank[:], func=TANH)


        left_values, left_q = {}, {}
        right_values, right_q = {}, {}
        right_rows = {}

        def left(h, g, part):
            values = four.tile([P, PART, T], BF16, name="left_values", align_bytes=64)
            left_values[h, g, part] = values
            cols = slice(PART * part, PART * part + PART)
            nc.vector.tensor_tensor(
                out=values[:].rearrange("p (f i) t -> p f t i", i=4),
                in0=act["x", h, g][:, :, cols].rearrange("p t (f i) -> p f t i", i=4),
                in1=factors["emph"][:, g, :].unsqueeze(1).unsqueeze(3).to_broadcast([P, PART // 4, T, 4]),
                op=MULT,
            )

        def quant_left(h, g, part):
            if (h, g) not in left_q:
                left_q[h, g] = codes_and_scales(GROUP, f"left_{h}{g}")
            codes, scales = left_q[h, g]
            cols = slice(PART * part, PART * part + PART)
            quantize(codes[:, cols], scales[:, cols], left_values[h, g, part][:].rearrange("p f t -> p (f t)"))

        def diff(h, g, pair):
            for t in (2 * pair, 2 * pair + 1):
                nc.vector.scalar_tensor_tensor(
                    out=act["n", h, g][:, t, :],
                    in0=act["n", h, g][:, t, :],
                    scalar=minus_gamma[:, T * g + t : T * g + t + 1],
                    in1=act["x", h, g][:, t, :],
                    op0=MULT,
                    op1=ADD,
                )

        def weigh_right(h, g):
            right_rows[h, g] = keep.tile([P, T, GROUP], BF16, name="right_rows", align_bytes=64)
            for t in range(T):
                nc.scalar.activation(
                    out=right_rows[h, g][:, t, :],
                    in_=act["n", h, g][:, t, :],
                    func=COPY,
                    scale=rho_f[:, T * g + t : T * g + t + 1],
                )

        def right(h, g):
            values = two.tile([P, GROUP, T], BF16, name="right_values", align_bytes=64)
            right_values[h, g] = values
            target = values[:].rearrange("p (s m) t -> p m t s", s=T)
            if (h, g) in right_rows:
                nc.vector.tensor_copy(out=target, in_=right_rows[h, g][:].rearrange("p t (m s) -> p m t s", s=T))
            else:
                nc.vector.tensor_tensor(
                    out=target,
                    in0=act["n", h, g][:].rearrange("p t (m s) -> p m t s", s=T),
                    in1=factors["rho"][:, g, :].unsqueeze(1).unsqueeze(3).to_broadcast([P, P, T, T]),
                    op=MULT,
                )

        def quant_right(h, g):
            right_q[h, g] = codes_and_scales(GROUP, f"right_{h}{g}")
            codes, scales = right_q[h, g]
            quantize(codes[:], scales[:], right_values[h, g][:].rearrange("p f t -> p (f t)"))


        def divide(engine, target, source):
            if engine == "s":
                nc.scalar.activation(out=target, in_=source, func=COPY, scale=1.0 / 32.0)
            else:
                nc.vector.tensor_scalar_mul(target, source, 1.0 / 32.0)

        def main(i, h, engine):
            bank = banks.tile([P, GROUP], F32, name="bank")
            cols = slice(P * (i % T), P * (i % T) + P)
            for g in range(GROUPS):
                multiply(bank[:], left_q[i // T, g], cols, right_q[h, g], slice(0, GROUP), g == 0, g == GROUPS - 1)
            result = five.tile([P, GROUP], F32, name="result", align_bytes=64)
            divide(
                engine,
                result[:].rearrange("p (m s) -> p m s", s=T),
                bank[:].rearrange("p (s m) -> p m s", s=T),
            )
            nc.sync.dma_start(out=out_0[P * i : P * i + P, GROUP * h : GROUP * h + GROUP], in_=result[:])

        p_values, p_q = {}, {}

        def flipped(h, i, engine):
            bank = banks.tile([P, T, P], F32, name="bank")
            m_cols = slice(P * (i % T), P * (i % T) + P)
            for s in range(T):
                s_cols = slice(P * s, P * s + P)
                for g in range(GROUPS):
                    multiply(bank[:, s, :], right_q[h, g], s_cols, left_q[i // T, g], m_cols, g == 0, g == GROUPS - 1)
            if (h, i // 2) not in p_values:
                p_values[h, i // 2] = four.tile([P, 2 * P, T], BF16, name="p_values", align_bytes=64)
            target = p_values[h, i // 2][:, P * (i % 2) : P * (i % 2) + P, :]
            divide(engine, target, bank[:].rearrange("p s m -> p m s"))

        def quant_p(h, part):
            half = part // 2
            if (h, half) not in p_q:
                p_q[h, half] = codes_and_scales(GROUP, f"p_{h}{half}")
            codes, scales = p_q[h, half]
            cols = slice(PART * (part % 2), PART * (part % 2) + PART)
            quantize(codes[:, cols], scales[:, cols], p_values[h, part][:].rearrange("p m s -> p (m s)"))

        def store_p(h, half):
            codes, scales = p_q[h, half]
            cols = slice(GROUP * half, GROUP * half + GROUP)
            words = out_1[h][:, cols, :].rearrange("p m t -> p (m t)")
            nc.sync.dma_start(out=words.bitcast(I32), in_=codes[:].bitcast(I32))
            for q in range(P // 32):
                nc.sync.dma_start(
                    out=out_2[h][4 * q : 4 * q + 4, cols].bitcast(I32),
                    in_=scales[32 * q : 32 * q + 4, :].bitcast(I32),
                )

        steps = {
            "prepare_factors": prepare_factors,
            "turn": turn,
            "quant_x": quant_x,
            "lay_w": lay_w,
            "quant_w": quant_w,
            "phi": phi,
            "left": left,
            "quant_left": quant_left,
            "diff": diff,
            "weigh_right": weigh_right,
            "right": right,
            "quant_right": quant_right,
            "main": main,
            "flipped": flipped,
            "quant_p": quant_p,
            "store_p": store_p,
        }
        ctx.enter_context(tc.manual_schedule())
        for name, *where in STEPS:
            steps[name](*where)
